import numpy as np, ml_dtypes
CORES = [24,48,72,152,176,200]
N = 6
import mx_ref
NC = 128
BF = ml_dtypes.bfloat16
def setup_inputs(rng):
    def f(*shape):
        return mx_ref.flush((rng.standard_normal(shape, dtype=np.float32) * np.exp2(rng.integers(-2, 3, shape[:-1] + (1,)))).astype(BF))
    return {"w": f(N, 128, 512), "x": f(N, 128, N * 4 * NC)}
def setup_inputs_blocks(rng):
    d = setup_inputs(rng)
    for k in ("w", "x"): d[k] = mx_ref.spread(d[k], rng, 2)
    return d
def setup_inputs_wide(rng):
    d = setup_inputs(rng)
    for k in ("w", "x"): d[k] = mx_ref.flush((d[k].astype(np.float32) * np.exp2(rng.integers(-8, 9, (N, 1, 1))).astype(np.float32)).astype(BF))
    return d
def setup_inputs_zeros(rng):
    d = setup_inputs(rng); v = d["x"].reshape(N, 128, -1, 4).copy()
    v[np.broadcast_to((rng.random((N, 1, v.shape[2], 1)) < 0.33), v.shape)] = 0
    d["x"] = v.reshape(d["x"].shape)
    return d
def reference(w, x):
    QW = [mx_ref.quantize(w[j]) for j in range(N)]
    y = np.zeros((N, 128, NC), np.float32)
    for r in range(N):
        for j in range(N):
            p = mx_ref.matmul(QW[j], mx_ref.quantize(x[j][:, 4 * NC * r:4 * NC * r + 4 * NC]))
            y[r] = p if j == 0 else y[r] + p
    return {"y": y}

@@ -1,0 +1,191 @@
+from concourse.bass import DstId, RemoteDMATransfer
+from concourse.mybir import dt
+
+N = 6
+HALF = N // 2
+TW = 128
+TB = 4 * TW
+PK = 2 * TW
+SIM_CORES = 256
+
+SCRATCH = {
+    "wb": ("sbuf", [128, TB], "bfloat16"),
+    "xb": ("sbuf", [128, N * TB], "bfloat16"),
+    "q": ("sbuf", [128, 9 * TW], "float8_e4m3fn_x4"),
+    "qs": ("sbuf", [128, 9 * TW], "uint8"),
+    "rq": ("sbuf", [128, (N - 1) * PK], "float8_e4m3fn_x4"),
+    "rs": ("sbuf", [128, (N - 1) * PK], "uint8"),
+    "acc": ("psum", [128, 512], "float32"),
+    "yb": ("sbuf", [128, TW], "float32"),
+}
+SEMAPHORES = ["ldw", "lda", "ldb", "q0", "q1", "q2", "q3", "hs", "hc", "sent", "mm", "cp", "st"] + [
+    "arr%d" % k for k in range(N - 1)]
+
+
+def _engines(mask):
+    return [1 << i for i in range(mask.bit_length()) if (mask >> i) & 1]
+
+
+def _slot(src, dst):
+    return src if src < dst else src - 1
+
+
+def _plan(cores, topo):
+    n = len(cores)
+    port = {}
+
+    def seen(d, die):
+        return port.get((d, die), 0)
+
+    def arrive(d, die):
+        port[(d, die)] = seen(d, die) + 1
+
+    plan = []
+    for s in range(n):
+        d = (s + HALF) % n
+        assert topo.may_write(cores[s], cores[d])
+        plan.append({"pairs": [], "direct": {"src": s, "dst": d, "via": None, "tile": 6, "xfirst": False, "turn": 1}})
+        arrive(d, topo.die(cores[s]))
+    for s in range(n):
+        c = cores[s]
+        chip = [k for k in range(SIM_CORES)
+                if k != c and topo.host(k) == topo.host(c) and topo.chip(k) == topo.chip(c)]
+        own = topo.die(c)
+        other = [topo.die(k) for k in chip if topo.die(k) != own][0]
+        near = [d for d in range(n) if d // HALF == s // HALF and d != s]
+        far = [d for d in range(n) if d // HALF != s // HALF and d != plan[s]["direct"]["dst"]]
+        chosen = []
+        for stage, (p, r) in enumerate((near, far)):
+            if max(seen(r, own), seen(p, other)) < max(seen(p, own), seen(r, other)):
+                p, r = r, p
+            arrive(p, own)
+            arrive(r, other)
+            a = {"src": s, "dst": p, "die": own, "tile": 3 * stage, "xfirst": True, "turn": 2 * stage}
+            b = {"src": s, "dst": r, "die": other, "tile": 3 * stage + 1, "xfirst": False, "turn": 2 * stage}
+            plan[s]["pairs"].append((a, b))
+            chosen += [a, b]
+        free = list(chip)
+        for f in sorted(chosen, key=lambda f: topo.may_write(c, cores[f["dst"]])):
+            k = [k for k in free if topo.die(k) == f["die"] and topo.may_write(k, cores[f["dst"]])][0]
+            f["via"] = k
+            free.remove(k)
+    return plan
+
+
+def _flows(plan):
+    out = []
+    for p in plan:
+        out.append(p["direct"])
+        for a, b in p["pairs"]:
+            out += [a, b]
+    return out
+
+
+def _tile(buf, t, k=1):
+    return buf[:, t * TW:(t + k) * TW]
+
+
+def _forward(g, core, T, topo, f):
+    dst = T.cores[f["dst"]]
+    rid, pid = topo.addr(dst, core)
+    mask = topo.mask(core, dst)
+    fed = len(_engines(topo.mask(T.cores[f["src"]], core))) // 2
+    lo = _slot(f["src"], f["dst"]) * PK
+    arr = T.sem["arr%d" % _slot(f["src"], f["dst"])]
+    g.wait_ge(T.sem.hs, fed)
+    g.remote_dma(T.rs[:, lo:lo + PK], T.rs[:, 0:PK], arr, T.sem.sent, pid, rid, mask)
+    g.wait_ge(T.sem.hc, fed)
+    g.remote_dma(T.rq[:, lo:lo + PK].bitcast(dt.uint8), T.rq[:, 0:PK].bitcast(dt.uint8), arr, T.sem.sent, pid, rid, mask)
+    g.wait_ge(T.sem.sent, 2 * len(_engines(mask)))
+
+
+def _rank(g, core, T, topo, plan, rank):
+    sem = T.sem
+    mine = plan[rank]
+    v, t = g.vector, g.tensor
+
+    lo = (rank // HALF) * HALF * TB
+    ol = HALF * TB - lo
+    g.sync.dma_start(T.wb[:], T.w[:]).then_inc(sem.ldw, 16)
+    g.scalar.dma_start(T.xb[:, lo:lo + HALF * TB], T.x[:, lo:lo + HALF * TB]).then_inc(sem.lda, 16)
+    g.sync.dma_start(T.xb[:, ol:ol + HALF * TB], T.x[:, ol:ol + HALF * TB]).then_inc(sem.ldb, 16)
+
+    def quant(tile, src, s):
+        v.quantize_mx(_tile(T.q, tile), _tile(T.qs, tile), src).then_inc(s, 1)
+
+    def xt(d):
+        return T.xb[:, d * TB:(d + 1) * TB]
+
+    (a, b), (c, d) = mine["pairs"]
+    e = mine["direct"]
+    v.wait_ge(sem.ldw, 16)
+    quant(1, T.wb[:], sem.q1)
+    quant(4, T.wb[:], sem.q2)
+    quant(6, T.wb[:], sem.q3)
+    v.wait_ge(sem.lda, 16)
+    quant(0, xt(a["dst"]), sem.q1)
+    quant(2, xt(b["dst"]), sem.q1)
+    quant(8, xt(rank), sem.q0)
+    v.wait_ge(sem.ldb, 16)
+    quant(3, xt(c["dst"]), sem.q2)
+    quant(5, xt(d["dst"]), sem.q2)
+    quant(7, xt(e["dst"]), sem.q3)
+
+    sent = 0
+    for ready, pair in ((sem.q1, (a, b)), (sem.q2, (c, d))):
+        g.wait_ge(ready, 3)
+        for codes in (False, True):
+            trs = []
+            for i, f in enumerate(pair):
+                rid, pid = topo.addr(f["via"], core)
+                m = sum(_engines(topo.mask(core, f["via"]))[1 - i::2])
+                if codes:
+                    src, dst = _tile(T.q, f["tile"], 2).bitcast(dt.uint8), T.rq[:, 0:PK].bitcast(dt.uint8)
+                else:
+                    src, dst = _tile(T.qs, f["tile"], 2), T.rs[:, 0:PK]
+                trs.append(RemoteDMATransfer(dst_ids=[DstId(rid=rid, pnc=pid)], dma_engine_mask=m,
+                                             remote_sem=sem.hc if codes else sem.hs, src=src, dst=dst))
+                sent += len(_engines(m))
+            g.remote_dma_fused(trs, local_sem=sem.sent)
+    peer = T.cores[e["dst"]]
+    rid, pid = topo.addr(peer, core)
+    m = topo.mask(core, peer)
+    at = _slot(rank, e["dst"]) * PK
+    arr = sem["arr%d" % _slot(rank, e["dst"])]
+    g.wait_ge(sem.q3, 2)
+    g.remote_dma(T.rs[:, at:at + PK], _tile(T.qs, e["tile"], 2), arr, sem.sent, pid, rid, m)
+    g.remote_dma(T.rq[:, at:at + PK].bitcast(dt.uint8), _tile(T.q, e["tile"], 2).bitcast(dt.uint8), arr, sem.sent,
+                 pid, rid, m)
+    sent += 2 * len(_engines(m))
+
+    out = T.acc[:, 0:TW]
+    t.wait_ge(sem.q1, 3)
+    t.wait_ge(sem.q0, 1)
+    t.matmul_mx(out, _tile(T.q, 1), _tile(T.qs, 1), _tile(T.q, 8), _tile(T.qs, 8), True, False)
+    inbound = sorted((f for f in _flows(plan) if f["dst"] == rank), key=lambda f: f["turn"])
+    for i, f in enumerate(inbound):
+        slot = _slot(f["src"], rank)
+        sender = T.cores[f["src"]] if f["via"] is None else f["via"]
+        xo, wo = (2 * slot, 2 * slot + 1) if f["xfirst"] else (2 * slot + 1, 2 * slot)
+        t.wait_ge(sem["arr%d" % slot], 2 * len(_engines(topo.mask(sender, core))))
+        mm = t.matmul_mx(out, _tile(T.rq, wo), _tile(T.rs, wo), _tile(T.rq, xo), _tile(T.rs, xo), False,
+                         i == len(inbound) - 1)
+    mm.then_inc(sem.mm, 1)
+
+    v.wait_ge(sem.mm, 1)
+    v.tensor_copy(T.yb[:], out).then_inc(sem.cp, 1)
+    g.sync.wait_ge(sem.cp, 1)
+    g.sync.dma_start(T.y[:], T.yb[:]).then_inc(sem.st, 16)
+    g.sync.wait_ge(sem.st, 16)
+    g.wait_ge(sem.sent, sent)
+
+
+def rank_program(g, core, T, topo):
+    plan = _plan(list(T.cores), topo)
+    rank = T.rank_of(core)
+    if rank is not None:
+        _rank(g, core, T, topo, plan, rank)
+        return
+    for f in _flows(plan):
+        if f["via"] == core:
+            _forward(g, core, T, topo, f)

@@ -18,7 +18,7 @@ SCRATCH = {
     "acc": ("psum", [128, 512], "float32"),
     "yb": ("sbuf", [128, TW], "float32"),
 }
-SEMAPHORES = ["ldw", "lda", "ldb", "q0", "q1", "q2", "q3", "hs", "hc", "sent", "mm", "cp", "st"] + [
+SEMAPHORES = ["ldw", "lda", "ldb", "qw", "q0", "q1", "q2", "q3", "hw", "hs", "hc", "sent", "mm", "cp", "st"] + [
     "arr%d" % k for k in range(N - 1)]
 
 
@@ -32,43 +32,36 @@ def _slot(src, dst):
 
 def _plan(cores, topo):
     n = len(cores)
-    port = {}
-
-    def seen(d, die):
-        return port.get((d, die), 0)
-
-    def arrive(d, die):
-        port[(d, die)] = seen(d, die) + 1
-
     plan = []
-    for s in range(n):
-        d = (s + HALF) % n
-        assert topo.may_write(cores[s], cores[d])
-        plan.append({"pairs": [], "direct": {"src": s, "dst": d, "via": None, "tile": 6, "xfirst": False, "turn": 1}})
-        arrive(d, topo.die(cores[s]))
     for s in range(n):
         c = cores[s]
         chip = [k for k in range(SIM_CORES)
                 if k != c and topo.host(k) == topo.host(c) and topo.chip(k) == topo.chip(c)]
         own = topo.die(c)
         other = [topo.die(k) for k in chip if topo.die(k) != own][0]
-        near = [d for d in range(n) if d // HALF == s // HALF and d != s]
-        far = [d for d in range(n) if d // HALF != s // HALF and d != plan[s]["direct"]["dst"]]
+        here = (s // HALF) * HALF
+        there = HALF - here
+
+        def peer(base, k):
+            return base + (s % HALF + k) % HALF
+
+        assert topo.may_write(c, cores[peer(there, 0)])
+        mine = {"pairs": [], "direct": {"src": s, "dst": peer(there, 0), "via": None, "tile": 6, "xfirst": False,
+                                        "turn": 3, "writes": 2}}
         chosen = []
-        for stage, (p, r) in enumerate((near, far)):
-            if max(seen(r, own), seen(p, other)) < max(seen(p, own), seen(r, other)):
-                p, r = r, p
-            arrive(p, own)
-            arrive(r, other)
-            a = {"src": s, "dst": p, "die": own, "tile": 3 * stage, "xfirst": True, "turn": 2 * stage}
-            b = {"src": s, "dst": r, "die": other, "tile": 3 * stage + 1, "xfirst": False, "turn": 2 * stage}
-            plan[s]["pairs"].append((a, b))
+        for stage, base in enumerate((here, there)):
+            a = {"src": s, "dst": peer(base, 1), "die": own, "tile": 3 * stage, "xfirst": True, "turn": 2 * stage,
+                 "writes": 2 + stage}
+            b = {"src": s, "dst": peer(base, 2), "die": other, "tile": 3 * stage + 1, "xfirst": False,
+                 "turn": 2 * stage, "writes": 2 + stage}
+            mine["pairs"].append((a, b))
             chosen += [a, b]
         free = list(chip)
         for f in sorted(chosen, key=lambda f: topo.may_write(c, cores[f["dst"]])):
             k = [k for k in free if topo.die(k) == f["die"] and topo.may_write(k, cores[f["dst"]])][0]
             f["via"] = k
             free.remove(k)
+        plan.append(mine)
     return plan
 
 
@@ -85,18 +78,30 @@ def _tile(buf, t, k=1):
     return buf[:, t * TW:(t + k) * TW]
 
 
+def _bytes(buf, t, k=1):
+    return _tile(buf, t, k).bitcast(dt.uint8)
+
+
 def _forward(g, core, T, topo, f):
     dst = T.cores[f["dst"]]
     rid, pid = topo.addr(dst, core)
     mask = topo.mask(core, dst)
     fed = len(_engines(topo.mask(T.cores[f["src"]], core))) // 2
-    lo = _slot(f["src"], f["dst"]) * PK
+    at = 2 * _slot(f["src"], f["dst"])
     arr = T.sem["arr%d" % _slot(f["src"], f["dst"])]
+    xo, wo = (0, 1) if f["xfirst"] else (1, 0)
+    apart = f["writes"] > 2
+    if apart:
+        g.wait_ge(T.sem.hw, fed)
+        g.remote_dma(_bytes(T.rq, at + wo), _bytes(T.rq, wo), arr, T.sem.sent, pid, rid, mask)
     g.wait_ge(T.sem.hs, fed)
-    g.remote_dma(T.rs[:, lo:lo + PK], T.rs[:, 0:PK], arr, T.sem.sent, pid, rid, mask)
+    g.remote_dma(_tile(T.rs, at, 2), _tile(T.rs, 0, 2), arr, T.sem.sent, pid, rid, mask)
     g.wait_ge(T.sem.hc, fed)
-    g.remote_dma(T.rq[:, lo:lo + PK].bitcast(dt.uint8), T.rq[:, 0:PK].bitcast(dt.uint8), arr, T.sem.sent, pid, rid, mask)
-    g.wait_ge(T.sem.sent, 2 * len(_engines(mask)))
+    if apart:
+        g.remote_dma(_bytes(T.rq, at + xo), _bytes(T.rq, xo), arr, T.sem.sent, pid, rid, mask)
+    else:
+        g.remote_dma(_bytes(T.rq, at, 2), _bytes(T.rq, 0, 2), arr, T.sem.sent, pid, rid, mask)
+    g.wait_ge(T.sem.sent, f["writes"] * len(_engines(mask)))
 
 
 def _rank(g, core, T, topo, plan, rank):
@@ -119,44 +124,50 @@ def _rank(g, core, T, topo, plan, rank):
     (a, b), (c, d) = mine["pairs"]
     e = mine["direct"]
     v.wait_ge(sem.ldw, 16)
+    quant(4, T.wb[:], sem.qw)
     quant(1, T.wb[:], sem.q1)
-    quant(4, T.wb[:], sem.q2)
-    quant(6, T.wb[:], sem.q3)
     v.wait_ge(sem.lda, 16)
     quant(0, xt(a["dst"]), sem.q1)
     quant(2, xt(b["dst"]), sem.q1)
-    quant(8, xt(rank), sem.q0)
     v.wait_ge(sem.ldb, 16)
     quant(3, xt(c["dst"]), sem.q2)
     quant(5, xt(d["dst"]), sem.q2)
+    quant(6, T.wb[:], sem.q3)
     quant(7, xt(e["dst"]), sem.q3)
+    quant(8, xt(rank), sem.q0)
 
-    sent = 0
-    for ready, pair in ((sem.q1, (a, b)), (sem.q2, (c, d))):
-        g.wait_ge(ready, 3)
-        for codes in (False, True):
-            trs = []
-            for i, f in enumerate(pair):
-                rid, pid = topo.addr(f["via"], core)
-                m = sum(_engines(topo.mask(core, f["via"]))[1 - i::2])
-                if codes:
-                    src, dst = _tile(T.q, f["tile"], 2).bitcast(dt.uint8), T.rq[:, 0:PK].bitcast(dt.uint8)
-                else:
-                    src, dst = _tile(T.qs, f["tile"], 2), T.rs[:, 0:PK]
-                trs.append(RemoteDMATransfer(dst_ids=[DstId(rid=rid, pnc=pid)], dma_engine_mask=m,
-                                             remote_sem=sem.hc if codes else sem.hs, src=src, dst=dst))
-                sent += len(_engines(m))
-            g.remote_dma_fused(trs, local_sem=sem.sent)
+    sent = [0]
+
+    def feed(pair, parts, remote):
+        trs = []
+        for i, (f, (src, dst)) in enumerate(zip(pair, parts)):
+            rid, pid = topo.addr(f["via"], core)
+            m = sum(_engines(topo.mask(core, f["via"]))[1 - i::2])
+            trs.append(RemoteDMATransfer(dst_ids=[DstId(rid=rid, pnc=pid)], dma_engine_mask=m, remote_sem=remote,
+                                         src=src, dst=dst))
+            sent[0] += len(_engines(m))
+        g.remote_dma_fused(trs, local_sem=sem.sent)
+
+    def where(f):
+        return (0, 1) if f["xfirst"] else (1, 0)
+
+    g.wait_ge(sem.qw, 1)
+    feed((c, d), [(_bytes(T.q, 4), _bytes(T.rq, where(f)[1])) for f in (c, d)], sem.hw)
+    g.wait_ge(sem.q1, 3)
+    feed((a, b), [(_tile(T.qs, f["tile"], 2), _tile(T.rs, 0, 2)) for f in (a, b)], sem.hs)
+    feed((a, b), [(_bytes(T.q, f["tile"], 2), _bytes(T.rq, 0, 2)) for f in (a, b)], sem.hc)
+    g.wait_ge(sem.q2, 2)
+    feed((c, d), [(_tile(T.qs, f["tile"], 2), _tile(T.rs, 0, 2)) for f in (c, d)], sem.hs)
+    feed((c, d), [(_bytes(T.q, f["tile"] + where(f)[0]), _bytes(T.rq, where(f)[0])) for f in (c, d)], sem.hc)
     peer = T.cores[e["dst"]]
     rid, pid = topo.addr(peer, core)
     m = topo.mask(core, peer)
-    at = _slot(rank, e["dst"]) * PK
+    at = 2 * _slot(rank, e["dst"])
     arr = sem["arr%d" % _slot(rank, e["dst"])]
     g.wait_ge(sem.q3, 2)
-    g.remote_dma(T.rs[:, at:at + PK], _tile(T.qs, e["tile"], 2), arr, sem.sent, pid, rid, m)
-    g.remote_dma(T.rq[:, at:at + PK].bitcast(dt.uint8), _tile(T.q, e["tile"], 2).bitcast(dt.uint8), arr, sem.sent,
-                 pid, rid, m)
-    sent += 2 * len(_engines(m))
+    g.remote_dma(_tile(T.rs, at, 2), _tile(T.qs, e["tile"], 2), arr, sem.sent, pid, rid, m)
+    g.remote_dma(_bytes(T.rq, at, 2), _bytes(T.q, e["tile"], 2), arr, sem.sent, pid, rid, m)
+    sent[0] += 2 * len(_engines(m))
 
     out = T.acc[:, 0:TW]
     t.wait_ge(sem.q1, 3)
@@ -167,7 +178,7 @@ def _rank(g, core, T, topo, plan, rank):
         slot = _slot(f["src"], rank)
         sender = T.cores[f["src"]] if f["via"] is None else f["via"]
         xo, wo = (2 * slot, 2 * slot + 1) if f["xfirst"] else (2 * slot + 1, 2 * slot)
-        t.wait_ge(sem["arr%d" % slot], 2 * len(_engines(topo.mask(sender, core))))
+        t.wait_ge(sem["arr%d" % slot], f["writes"] * len(_engines(topo.mask(sender, core))))
         mm = t.matmul_mx(out, _tile(T.rq, wo), _tile(T.rs, wo), _tile(T.rq, xo), _tile(T.rs, xo), False,
                          i == len(inbound) - 1)
     mm.then_inc(sem.mm, 1)
@@ -177,7 +188,7 @@ def _rank(g, core, T, topo, plan, rank):
     g.sync.wait_ge(sem.cp, 1)
     g.sync.dma_start(T.y[:], T.yb[:]).then_inc(sem.st, 16)
     g.sync.wait_ge(sem.st, 16)
-    g.wait_ge(sem.sent, sent)
+    g.wait_ge(sem.sent, sent[0])
 
 
 def rank_program(g, core, T, topo):

from concourse.bass import DstId, RemoteDMATransfer
from concourse.mybir import dt

N = 6
HALF = N // 2
TW = 128
TB = 4 * TW
PK = 2 * TW
SIM_CORES = 256

SCRATCH = {
    "wb": ("sbuf", [128, TB], "bfloat16"),
    "xb": ("sbuf", [128, N * TB], "bfloat16"),
    "q": ("sbuf", [128, 9 * TW], "float8_e4m3fn_x4"),
    "qs": ("sbuf", [128, 9 * TW], "uint8"),
    "rq": ("sbuf", [128, (N - 1) * PK], "float8_e4m3fn_x4"),
    "rs": ("sbuf", [128, (N - 1) * PK], "uint8"),
    "acc": ("psum", [128, 512], "float32"),
    "yb": ("sbuf", [128, TW], "float32"),
}
SEMAPHORES = ["ldw", "lda", "ldb", "qw", "q0", "q1", "q2", "q3", "hw", "hs", "hc", "sent", "mm", "cp", "st"] + [
    "arr%d" % k for k in range(N - 1)]


def _engines(mask):
    return [1 << i for i in range(mask.bit_length()) if (mask >> i) & 1]


def _slot(src, dst):
    return src if src < dst else src - 1


def _plan(cores, topo):
    n = len(cores)
    plan = []
    for s in range(n):
        c = cores[s]
        chip = [k for k in range(SIM_CORES)
                if k != c and topo.host(k) == topo.host(c) and topo.chip(k) == topo.chip(c)]
        own = topo.die(c)
        other = [topo.die(k) for k in chip if topo.die(k) != own][0]
        here = (s // HALF) * HALF
        there = HALF - here

        def peer(base, k):
            return base + (s % HALF + k) % HALF

        assert topo.may_write(c, cores[peer(there, 0)])
        mine = {"pairs": [], "direct": {"src": s, "dst": peer(there, 0), "via": None, "tile": 6, "xfirst": False,
                                        "turn": 3, "writes": 2}}
        chosen = []
        for stage, base in enumerate((here, there)):
            a = {"src": s, "dst": peer(base, 1), "die": own, "tile": 3 * stage, "xfirst": True, "turn": 2 * stage,
                 "writes": 2 + stage}
            b = {"src": s, "dst": peer(base, 2), "die": other, "tile": 3 * stage + 1, "xfirst": False,
                 "turn": 2 * stage, "writes": 2 + stage}
            mine["pairs"].append((a, b))
            chosen += [a, b]
        free = list(chip)
        for f in sorted(chosen, key=lambda f: topo.may_write(c, cores[f["dst"]])):
            k = [k for k in free if topo.die(k) == f["die"] and topo.may_write(k, cores[f["dst"]])][0]
            f["via"] = k
            free.remove(k)
        plan.append(mine)
    return plan


def _flows(plan):
    out = []
    for p in plan:
        out.append(p["direct"])
        for a, b in p["pairs"]:
            out += [a, b]
    return out


def _tile(buf, t, k=1):
    return buf[:, t * TW:(t + k) * TW]


def _bytes(buf, t, k=1):
    return _tile(buf, t, k).bitcast(dt.uint8)


def _forward(g, core, T, topo, f):
    dst = T.cores[f["dst"]]
    rid, pid = topo.addr(dst, core)
    mask = topo.mask(core, dst)
    fed = len(_engines(topo.mask(T.cores[f["src"]], core))) // 2
    at = 2 * _slot(f["src"], f["dst"])
    arr = T.sem["arr%d" % _slot(f["src"], f["dst"])]
    xo, wo = (0, 1) if f["xfirst"] else (1, 0)
    apart = f["writes"] > 2
    if apart:
        g.wait_ge(T.sem.hw, fed)
        g.remote_dma(_bytes(T.rq, at + wo), _bytes(T.rq, wo), arr, T.sem.sent, pid, rid, mask)
    g.wait_ge(T.sem.hs, fed)
    g.remote_dma(_tile(T.rs, at, 2), _tile(T.rs, 0, 2), arr, T.sem.sent, pid, rid, mask)
    g.wait_ge(T.sem.hc, fed)
    if apart:
        g.remote_dma(_bytes(T.rq, at + xo), _bytes(T.rq, xo), arr, T.sem.sent, pid, rid, mask)
    else:
        g.remote_dma(_bytes(T.rq, at, 2), _bytes(T.rq, 0, 2), arr, T.sem.sent, pid, rid, mask)
    g.wait_ge(T.sem.sent, f["writes"] * len(_engines(mask)))


def _rank(g, core, T, topo, plan, rank):
    sem = T.sem
    mine = plan[rank]
    v, t = g.vector, g.tensor

    lo = (rank // HALF) * HALF * TB
    ol = HALF * TB - lo
    g.sync.dma_start(T.wb[:], T.w[:]).then_inc(sem.ldw, 16)
    g.scalar.dma_start(T.xb[:, lo:lo + HALF * TB], T.x[:, lo:lo + HALF * TB]).then_inc(sem.lda, 16)
    g.sync.dma_start(T.xb[:, ol:ol + HALF * TB], T.x[:, ol:ol + HALF * TB]).then_inc(sem.ldb, 16)

    def quant(tile, src, s):
        v.quantize_mx(_tile(T.q, tile), _tile(T.qs, tile), src).then_inc(s, 1)

    def xt(d):
        return T.xb[:, d * TB:(d + 1) * TB]

    (a, b), (c, d) = mine["pairs"]
    e = mine["direct"]
    v.wait_ge(sem.ldw, 16)
    quant(4, T.wb[:], sem.qw)
    quant(1, T.wb[:], sem.q1)
    v.wait_ge(sem.lda, 16)
    quant(0, xt(a["dst"]), sem.q1)
    quant(2, xt(b["dst"]), sem.q1)
    v.wait_ge(sem.ldb, 16)
    quant(3, xt(c["dst"]), sem.q2)
    quant(5, xt(d["dst"]), sem.q2)
    quant(6, T.wb[:], sem.q3)
    quant(7, xt(e["dst"]), sem.q3)
    quant(8, xt(rank), sem.q0)

    sent = [0]

    def feed(pair, parts, remote):
        trs = []
        for i, (f, (src, dst)) in enumerate(zip(pair, parts)):
            rid, pid = topo.addr(f["via"], core)
            m = sum(_engines(topo.mask(core, f["via"]))[1 - i::2])
            trs.append(RemoteDMATransfer(dst_ids=[DstId(rid=rid, pnc=pid)], dma_engine_mask=m, remote_sem=remote,
                                         src=src, dst=dst))
            sent[0] += len(_engines(m))
        g.remote_dma_fused(trs, local_sem=sem.sent)

    def where(f):
        return (0, 1) if f["xfirst"] else (1, 0)

    g.wait_ge(sem.qw, 1)
    feed((c, d), [(_bytes(T.q, 4), _bytes(T.rq, where(f)[1])) for f in (c, d)], sem.hw)
    g.wait_ge(sem.q1, 3)
    feed((a, b), [(_tile(T.qs, f["tile"], 2), _tile(T.rs, 0, 2)) for f in (a, b)], sem.hs)
    feed((a, b), [(_bytes(T.q, f["tile"], 2), _bytes(T.rq, 0, 2)) for f in (a, b)], sem.hc)
    g.wait_ge(sem.q2, 2)
    feed((c, d), [(_tile(T.qs, f["tile"], 2), _tile(T.rs, 0, 2)) for f in (c, d)], sem.hs)
    feed((c, d), [(_bytes(T.q, f["tile"] + where(f)[0]), _bytes(T.rq, where(f)[0])) for f in (c, d)], sem.hc)
    peer = T.cores[e["dst"]]
    rid, pid = topo.addr(peer, core)
    m = topo.mask(core, peer)
    at = 2 * _slot(rank, e["dst"])
    arr = sem["arr%d" % _slot(rank, e["dst"])]
    g.wait_ge(sem.q3, 2)
    g.remote_dma(_tile(T.rs, at, 2), _tile(T.qs, e["tile"], 2), arr, sem.sent, pid, rid, m)
    g.remote_dma(_bytes(T.rq, at, 2), _bytes(T.q, e["tile"], 2), arr, sem.sent, pid, rid, m)
    sent[0] += 2 * len(_engines(m))

    out = T.acc[:, 0:TW]
    t.wait_ge(sem.q1, 3)
    t.wait_ge(sem.q0, 1)
    t.matmul_mx(out, _tile(T.q, 1), _tile(T.qs, 1), _tile(T.q, 8), _tile(T.qs, 8), True, False)
    inbound = sorted((f for f in _flows(plan) if f["dst"] == rank), key=lambda f: f["turn"])
    for i, f in enumerate(inbound):
        slot = _slot(f["src"], rank)
        sender = T.cores[f["src"]] if f["via"] is None else f["via"]
        xo, wo = (2 * slot, 2 * slot + 1) if f["xfirst"] else (2 * slot + 1, 2 * slot)
        t.wait_ge(sem["arr%d" % slot], f["writes"] * len(_engines(topo.mask(sender, core))))
        mm = t.matmul_mx(out, _tile(T.rq, wo), _tile(T.rs, wo), _tile(T.rq, xo), _tile(T.rs, xo), False,
                         i == len(inbound) - 1)
    mm.then_inc(sem.mm, 1)

    v.wait_ge(sem.mm, 1)
    v.tensor_copy(T.yb[:], out).then_inc(sem.cp, 1)
    g.sync.wait_ge(sem.cp, 1)
    g.sync.dma_start(T.y[:], T.yb[:]).then_inc(sem.st, 16)
    g.sync.wait_ge(sem.st, 16)
    g.wait_ge(sem.sent, sent[0])


def rank_program(g, core, T, topo):
    plan = _plan(list(T.cores), topo)
    rank = T.rank_of(core)
    if rank is not None:
        _rank(g, core, T, topo, plan, rank)
        return
    for f in _flows(plan):
        if f["via"] == core:
            _forward(g, core, T, topo, f)
